import numpy as np
import ml_dtypes


def mxq(x, axis, fmt="e4m3"):
    dtype, down = {"e4m3": (ml_dtypes.float8_e4m3fn, 7), "e5m2": (ml_dtypes.float8_e5m2, 14)}[fmt]
    v = np.moveaxis(np.asarray(x, np.float32).astype(ml_dtypes.bfloat16).astype(np.float64), axis, -1)
    blocks = v.reshape(v.shape[:-1] + (-1, 32))
    amax = np.abs(blocks).max(-1, keepdims=True)
    byte = np.maximum(np.where(amax > 0, np.frexp(amax)[1] - 1 + 127, 0) - down, 1)
    scale = np.exp2(byte - 127.0)
    codes = (blocks / scale).astype(np.float32).astype(dtype).astype(np.float64)
    return np.moveaxis((codes * scale).reshape(v.shape), -1, axis)


WIDE = False


def mx_kscale(k):
    if not WIDE:
        return np.ones(k)
    levels = np.array([10, -10, 5, -5, 0])
    if k % 512:
        return np.exp2(np.random.permutation(np.resize(levels, k // 32))).repeat(32)
    a = np.empty((k // 512, 16))
    for p in range(k // 512):
        a[p, :8] = np.random.permutation(np.resize(levels, 8))
        for g in range(8):
            far = levels[np.abs(levels - a[p, g]) >= 10]
            a[p, g + 8] = far[np.random.randint(len(far))]
    return np.exp2(a.ravel()).repeat(32)


def f64(x):
    return np.asarray(x).astype(np.float64)


def striped8(idx):
    return np.asarray(idx).reshape(8, -1, 16).transpose(0, 2, 1).reshape(128, -1).astype(np.uint16)


def unstriped8(offs):
    return offs.reshape(8, 16, -1).transpose(0, 2, 1).reshape(8, -1).astype(np.int64)


def pick8(x, idx, run):
    r = np.arange(len(x))
    return x[r[:, None], idx[r % (8 * run) // run]]


E2M1 = np.array([0.0, 0.5, 1.0, 1.5, 2.0, 3.0, 4.0, 6.0, -0.0, -0.5, -1.0, -1.5, -2.0, -3.0, -4.0, -6.0])


def pack_weight(w, fmt):
    k, n = w.shape
    w = f64(np.asarray(w, np.float32).astype(ml_dtypes.bfloat16)).reshape(k // 32, 32, n)
    amax = np.abs(w).max(1)
    if fmt == "e4m3":
        byte = np.frexp(amax)[1] - 1 + 127 - 7
    else:
        mant, ex = np.frexp(amax / 6.0)
        byte = np.where(mant > 0.5, ex, ex - 1) + 127
    byte = np.clip(np.where(amax > 0, byte, 1), 1, 254)
    scaled = (w * np.exp2(127.0 - byte)[:, None, :]).reshape(k, n).astype(np.float32)
    by_word = np.ascontiguousarray(scaled.reshape(k // 512, 128, 4, n).transpose(0, 1, 3, 2))
    if fmt == "e4m3":
        words = by_word.astype(ml_dtypes.float8_e4m3fn).view(np.uint8)
    else:
        c = by_word.astype(ml_dtypes.float4_e2m1fn).view(np.uint8) & 0xF
        words = (c[..., 0::2] | (c[..., 1::2] << 4)).reshape(k // 512, 128, 2 * n)
    return np.ascontiguousarray(words), np.ascontiguousarray(byte.astype(np.uint8).reshape(k // 512, 16, n))


def unpack_weight(words, scales, fmt):
    g, _, n = scales.shape
    words = np.ascontiguousarray(words).reshape(g, 128, n, -1)
    if fmt == "e4m3":
        vals = words.view(ml_dtypes.float8_e4m3fn).astype(np.float64)
    else:
        nib = np.empty((g, 128, n, 4), np.uint8)
        nib[..., 0::2] = words & 0xF
        nib[..., 1::2] = words >> 4
        vals = E2M1[nib]
    vals = vals * np.repeat(np.exp2(scales.astype(np.float64) - 127.0), 8, axis=1)[..., None]
    return vals.transpose(0, 1, 3, 2).reshape(g * 512, n)


def bf(x):
    return np.asarray(x, np.float32).astype(ml_dtypes.bfloat16)


def planes(Y):
    r, m = Y.shape
    b = f64(bf(Y)).reshape(r // 32, 32, m)
    amax = np.abs(b).max(1)
    byte = np.clip(np.where(amax > 0, np.frexp(amax)[1] - 1 + 127 - 7, 1), 1, 254)
    codes = (b * np.exp2(127.0 - byte)[:, None, :]).reshape(r, m).astype(np.float32).astype(ml_dtypes.float8_e4m3fn).view(np.uint8)
    words = codes.reshape(r // 512, 128, 4, m).transpose(0, 1, 3, 2)
    return np.ascontiguousarray(words), np.ascontiguousarray(byte.astype(np.uint8).reshape(r // 512, 16, m))


K, L, S, T, N = 1024, 512, 512, 512, 512


def setup_inputs():
    n = np.random.standard_normal
    idx = np.stack([np.random.randint(0, S, T) for _ in range(8)])
    idx2 = np.stack([np.random.randint(0, S, T) for _ in range(8)])
    fk = mx_kscale(K)
    fl = mx_kscale(L)
    xap = pack_weight(n((K, S)) / fk[:, None], "e2m1")
    wap = pack_weight(n((K, N)) * 1 / np.sqrt(K) * fk[:, None], "e4m3")
    wbp = pack_weight(n((L, N)) * 1 / np.sqrt(L) * fl[:, None], "e2m1")
    return {
        "xa_words": xap[0],
        "xa_scales": xap[1],
        "wa_words": wap[0],
        "wa_scales": wap[1],
        "xb": (n((L, S)) / fl[:, None]).astype(np.float32),
        "wb_words": wbp[0],
        "wb_scales": wbp[1],
        "ga": (np.random.uniform(0.3, 1.0, (1, T))).astype(np.float32),
        "gb": (np.random.uniform(0.3, 1.0, (1, T))).astype(np.float32),
        "offs": striped8(idx),
        "offs2": striped8(idx2),
    }


def reference(xa_words, xa_scales, wa_words, wa_scales, xb, wb_words, wb_scales, ga, gb, offs, offs2):
    idx = unstriped8(offs)
    idx2 = unstriped8(offs2)
    xau = unpack_weight(xa_words, xa_scales, "e2m1")
    wau = unpack_weight(wa_words, wa_scales, "e4m3")
    wbu = unpack_weight(wb_words, wb_scales, "e2m1")
    za = wau.T @ xau
    xbq = mxq(f64(xb), 0, "e4m3")
    zb = wbu.T @ xbq
    y = f64(ga) * pick8(za, idx, 64) + f64(gb) * pick8(zb, idx2, 64)
    words, scales = planes(y)
    return y, words, scales

@@ -1,0 +1,205 @@
+from contextlib import ExitStack
+
+import concourse.mybir as mybir
+
+F32 = mybir.dt.float32
+BF16 = mybir.dt.bfloat16
+I32 = mybir.dt.int32
+U16 = mybir.dt.uint16
+U8 = mybir.dt.uint8
+FP8X4 = mybir.dt.float8_e4m3fn_x4
+FP4X4 = mybir.dt.float4_e2m1fn_x4
+MULT = mybir.AluOpType.mult
+ADD = mybir.AluOpType.add
+
+P = 128
+PACK = 4
+K, L, S, T, N = 1024, 512, 512, 512, 512
+PASSES_A = K // (P * PACK)
+HALF = S // 2
+VECTOR_SHARE = 160
+CHUNKS = ((0, 384), (384, 128))
+
+FLOPS = 2 * (K + L) * S * N
+
+
+def load_scale_rows(nc, plane, scales):
+    for q in range(4):
+        nc.sync.dma_start(
+            out=plane[32 * q : 32 * q + 4, :, :].bitcast(I32),
+            in_=scales[:, 4 * q : 4 * q + 4, :].rearrange("z r c -> r z c").bitcast(I32),
+        )
+
+
+def tile_moe_heads_combine_two_buffers_pl_kernel(
+    tc, xa_words, xa_scales, wa_words, wa_scales, xb, wb_words, wb_scales, ga, gb, offs, offs2, out_0, out_1, out_2
+):
+    nc = tc.nc
+    with ExitStack() as ctx:
+        keep = ctx.enter_context(tc.tile_pool(name="keep", bufs=1))
+        psum = ctx.enter_context(tc.psum_pool(name="psum", bufs=1))
+
+        lists_a = keep.tile([P, T // 16], U16, name="lists_a")
+        lists_b = keep.tile([P, T // 16], U16, name="lists_b")
+        wa_raw = keep.tile([P, PASSES_A, N], I32, name="wa_raw", align_bytes=64)
+        wa_scale_raw = keep.tile([P, PASSES_A, N], U8, name="wa_scale_raw", align_bytes=64)
+        wa_codes = keep.tile([P, PACK, PASSES_A, P], I32, name="wa_codes", align_bytes=64)
+        wa_scale = keep.tile([P, PACK, PASSES_A, P], U8, name="wa_scale", align_bytes=64)
+        xa_codes = keep.tile([P, PASSES_A, 2 * S], U8, name="xa_codes", align_bytes=64)
+        xa_scale = keep.tile([P, PASSES_A, S], U8, name="xa_scale", align_bytes=64)
+        wb_raw = keep.tile([P, 2 * N], U8, name="wb_raw", align_bytes=64)
+        wb_scale_raw = keep.tile([P, 1, N], U8, name="wb_scale_raw", align_bytes=64)
+        wb_codes = keep.tile([P, PACK, 2 * P], U8, name="wb_codes", align_bytes=64)
+        wb_scale = keep.tile([P, PACK, P], U8, name="wb_scale", align_bytes=64)
+        xb_raw = [keep.tile([P, PACK, HALF], F32, name=f"xb_raw{h}", align_bytes=64) for h in range(2)]
+        xb_bf = [keep.tile([P, HALF, PACK], BF16, name=f"xb_bf{h}", align_bytes=64) for h in range(2)]
+        xb_codes = keep.tile([P, S], I32, name="xb_codes", align_bytes=64)
+        xb_scale = keep.tile([P, S], U8, name="xb_scale", align_bytes=64)
+        gate_a = keep.tile([P, T], F32, name="gate_a", align_bytes=64)
+        gate_b = keep.tile([P, T], F32, name="gate_b", align_bytes=64)
+        za = [keep.tile([P, S], F32, name=f"za{t}", align_bytes=64) for t in range(PACK)]
+        zb = [keep.tile([P, S], F32, name=f"zb{t}", align_bytes=64) for t in range(PACK)]
+        ya = [keep.tile([P, PACK, w], F32, name=f"ya{c}", align_bytes=64) for c, (a, w) in enumerate(CHUNKS)]
+        yb = [keep.tile([P, PACK, w], F32, name=f"yb{c}", align_bytes=64) for c, (a, w) in enumerate(CHUNKS)]
+        y = [keep.tile([P, PACK, w], F32, name=f"y{c}", align_bytes=64) for c, (a, w) in enumerate(CHUNKS)]
+        y_bf = [keep.tile([P, w, PACK], BF16, name=f"y_bf{c}", align_bytes=64) for c, (a, w) in enumerate(CHUNKS)]
+        y_codes = keep.tile([P, T], I32, name="y_codes", align_bytes=64)
+        y_scale = keep.tile([P, T], U8, name="y_scale", align_bytes=64)
+        first_half = psum.tile([P, S], F32, name="first_half", tag="bank_a3")
+        whole_b = [psum.tile([P, S], F32, name=f"bank_b{t}") for t in range(PACK)]
+        bank_b = [[whole_b[t][:, 0:HALF], whole_b[t][:, HALF:S]] for t in range(PACK)]
+        bank_b[0] = [first_half[:, 0:HALF], whole_b[0][:, HALF:S]]
+        bank_a = [psum.tile([P, S], F32, name=f"bank_a{t}", tag=f"bank_a{t}") for t in range(PACK)]
+
+        for plane in (wb_scale_raw, wa_scale_raw, xa_scale):
+            nc.vector.memset(plane[:].bitcast(I32), 0)
+
+        xb_rows = xb.rearrange("(p j) s -> p j s", j=PACK)
+        nc.sync.dma_start(out=xb_raw[0][:], in_=xb_rows[:, :, 0:HALF])
+        nc.sync.dma_start(out=wb_raw[:].bitcast(I32), in_=wb_words[0].bitcast(I32))
+        load_scale_rows(nc, wb_scale_raw, wb_scales)
+        nc.sync.dma_start(out=xb_raw[1][:], in_=xb_rows[:, :, HALF:S])
+        nc.sync.dma_start(lists_b[:], offs2)
+        nc.sync.dma_start(out=wa_raw[:], in_=wa_words.rearrange("z p c r -> p z (c r)").bitcast(I32))
+        load_scale_rows(nc, wa_scale_raw, wa_scales)
+        nc.sync.dma_start(out=gate_b[:], in_=gb[0].partition_broadcast(P))
+        nc.sync.dma_start(out=xa_codes[:].bitcast(I32), in_=xa_words.rearrange("z p c -> p z c").bitcast(I32))
+        load_scale_rows(nc, xa_scale, xa_scales)
+        nc.sync.dma_start(lists_a[:], offs)
+        nc.sync.dma_start(out=gate_a[:], in_=ga[0].partition_broadcast(P))
+
+        def round_xb(h, lo, hi, copy):
+            copy(
+                out=xb_bf[h][:, lo:hi, :].rearrange("p (c i) j -> p c j i", i=4),
+                in_=xb_raw[h][:, :, lo:hi].rearrange("p j (c i) -> p c j i", i=4),
+            )
+
+        def quantize_xb(h):
+            cols = slice(h * HALF, (h + 1) * HALF)
+            nc.vector.quantize_mx(
+                out=xb_codes[:, cols].bitcast(FP8X4),
+                scales=xb_scale[:, cols],
+                in_=xb_bf[h][:].rearrange("p s j -> p (s j)"),
+            )
+
+        def product_a(t):
+            for z in range(PASSES_A):
+                nc.tensor.matmul_mx(
+                    out=bank_a[t][:],
+                    lhsT=wa_codes[:, t, z, :].bitcast(FP8X4),
+                    lhsT_scale=wa_scale[:, t, z, :],
+                    rhs=xa_codes[:, z, :].bitcast(FP4X4),
+                    rhs_scale=xa_scale[:, z, :],
+                    start=(z == 0),
+                    stop=(z == PASSES_A - 1),
+                )
+            nc.scalar.copy(out=za[t][:], in_=bank_a[t][:])
+
+        def product_b(t, h):
+            cols = slice(h * HALF, (h + 1) * HALF)
+            nc.tensor.matmul_mx(
+                out=bank_b[t][h],
+                lhsT=wb_codes[:, t, :].bitcast(FP4X4),
+                lhsT_scale=wb_scale[:, t, :],
+                rhs=xb_codes[:, cols].bitcast(FP8X4),
+                rhs_scale=xb_scale[:, cols],
+                start=True,
+                stop=True,
+            )
+
+        def look_up(dst, table, lists, gate, c, t):
+            a, w = CHUNKS[c]
+            nc.vector.tensor_tensor(
+                dst[c][:, t, :], table[t][:].indirect(lists[:, a // 16 : (a + w) // 16]), gate[:, a : a + w], MULT
+            )
+
+        def combine(c):
+            a, w = CHUNKS[c]
+            nc.vector.tensor_tensor(y[c][:], ya[c][:], yb[c][:], ADD)
+            nc.sync.dma_start(out=out_0.rearrange("(p t) c -> p t c", t=PACK)[:, :, a : a + w], in_=y[c][:])
+            nc.scalar.copy(
+                out=y_bf[c][:].rearrange("p (c i) t -> p c t i", i=4),
+                in_=y[c][:].rearrange("p t (c i) -> p c t i", i=4),
+            )
+
+        def quantize_y(c):
+            a, w = CHUNKS[c]
+            flat = y_bf[c][:].rearrange("p c t -> p (c t)")
+            lo = 0
+            while lo < w:
+                n = 256 if w - lo >= 256 else 128
+                nc.vector.quantize_mx(
+                    out=y_codes[:, a + lo : a + lo + n].bitcast(FP8X4),
+                    scales=y_scale[:, a + lo : a + lo + n],
+                    in_=flat[:, PACK * lo : PACK * (lo + n)],
+                )
+                lo = lo + n
+            nc.sync.dma_start(
+                out=out_1[0].rearrange("p c r -> p (c r)").bitcast(I32)[:, a : a + w], in_=y_codes[:, a : a + w]
+            )
+
+        round_xb(0, 0, HALF, nc.vector.tensor_copy)
+        nc.vector.tensor_copy(
+            out=wb_codes[:].bitcast(U16).rearrange("p t (c i) -> p c t i", i=8),
+            in_=wb_raw[:].bitcast(U16).rearrange("p (c i t) -> p c t i", i=8, t=PACK),
+        )
+        quantize_xb(0)
+        nc.vector.tensor_copy(
+            out=wb_scale[:].rearrange("p t (c i) -> p c t i", i=16),
+            in_=wb_scale_raw[:, 0, :].rearrange("p (c i t) -> p c t i", i=16, t=PACK),
+        )
+        for t in range(PACK):
+            product_b(t, 0)
+        round_xb(1, 0, VECTOR_SHARE, nc.vector.tensor_copy)
+        round_xb(1, VECTOR_SHARE, HALF, nc.scalar.copy)
+        nc.scalar.copy(out=zb[0][:, 0:HALF], in_=bank_b[0][0])
+        quantize_xb(1)
+        for t in range(PACK):
+            product_b(t, 1)
+        nc.scalar.copy(out=zb[0][:, HALF:S], in_=bank_b[0][1])
+        for t in range(1, PACK):
+            nc.scalar.copy(out=zb[t][:], in_=whole_b[t][:])
+        nc.vector.tensor_copy(
+            out=wa_codes[:].rearrange("p t z (c i) -> p z c t i", i=4),
+            in_=wa_raw[:].rearrange("p z (c i t) -> p z c t i", i=4, t=PACK),
+        )
+        nc.vector.tensor_copy(
+            out=wa_scale[:].rearrange("p t z (c i) -> p z c t i", i=16),
+            in_=wa_scale_raw[:].rearrange("p z (c i t) -> p z c t i", i=16, t=PACK),
+        )
+        for t in range(PACK):
+            product_a(t)
+        for t in range(PACK):
+            for c in range(len(CHUNKS)):
+                look_up(yb, zb, lists_b, gate_b, c, t)
+        for c in range(len(CHUNKS)):
+            for t in range(PACK):
+                look_up(ya, za, lists_a, gate_a, c, t)
+            combine(c)
+        for c in range(len(CHUNKS)):
+            quantize_y(c)
+        for q in range(4):
+            queue = nc.scalar if q % 2 else nc.sync
+            queue.dma_start(
+                out=out_2[0, 4 * q : 4 * q + 4, :].bitcast(I32), in_=y_scale[32 * q : 32 * q + 4, :].bitcast(I32)
+            )

@@ -1,6 +1,7 @@
 from contextlib import ExitStack
 
 import concourse.mybir as mybir
+from concourse.masks import make_identity
 
 F32 = mybir.dt.float32
 BF16 = mybir.dt.bfloat16
@@ -37,44 +38,58 @@ def tile_moe_heads_combine_two_buffers_pl_kernel(
     nc = tc.nc
     with ExitStack() as ctx:
         keep = ctx.enter_context(tc.tile_pool(name="keep", bufs=1))
+        reuse = ctx.enter_context(tc.tile_pool(name="reuse", bufs=1))
         psum = ctx.enter_context(tc.psum_pool(name="psum", bufs=1))
 
         lists_a = keep.tile([P, T // 16], U16, name="lists_a")
         lists_b = keep.tile([P, T // 16], U16, name="lists_b")
         wa_raw = keep.tile([P, PASSES_A, N], I32, name="wa_raw", align_bytes=64)
         wa_scale_raw = keep.tile([P, PASSES_A, N], U8, name="wa_scale_raw", align_bytes=64)
-        wa_codes = keep.tile([P, PACK, PASSES_A, P], I32, name="wa_codes", align_bytes=64)
-        wa_scale = keep.tile([P, PACK, PASSES_A, P], U8, name="wa_scale", align_bytes=64)
         xa_codes = keep.tile([P, PASSES_A, 2 * S], U8, name="xa_codes", align_bytes=64)
         xa_scale = keep.tile([P, PASSES_A, S], U8, name="xa_scale", align_bytes=64)
         wb_raw = keep.tile([P, 2 * N], U8, name="wb_raw", align_bytes=64)
-        wb_scale_raw = keep.tile([P, 1, N], U8, name="wb_scale_raw", align_bytes=64)
+        wb_scale_raw = reuse.tile([P, 1, N], U8, name="wb_scale_raw", align_bytes=64, offset=0)
         wb_codes = keep.tile([P, PACK, 2 * P], U8, name="wb_codes", align_bytes=64)
-        wb_scale = keep.tile([P, PACK, P], U8, name="wb_scale", align_bytes=64)
         xb_raw = [keep.tile([P, PACK, HALF], F32, name=f"xb_raw{h}", align_bytes=64) for h in range(2)]
-        xb_bf = [keep.tile([P, HALF, PACK], BF16, name=f"xb_bf{h}", align_bytes=64) for h in range(2)]
+        xb_bf = [
+            keep.tile([P, HALF, PACK], BF16, name="xb_bf0", align_bytes=64),
+            reuse.tile([P, HALF, PACK], BF16, name="xb_bf1", align_bytes=64, offset=0),
+        ]
+        wa_scale = reuse.tile([P, PACK, PASSES_A, P], U8, name="wa_scale", align_bytes=64, offset=0)
+        wa_codes = reuse.tile([P, PACK, PASSES_A, P], I32, name="wa_codes", align_bytes=64, offset=1024)
         xb_codes = keep.tile([P, S], I32, name="xb_codes", align_bytes=64)
         xb_scale = keep.tile([P, S], U8, name="xb_scale", align_bytes=64)
         gate_a = keep.tile([P, T], F32, name="gate_a", align_bytes=64)
         gate_b = keep.tile([P, T], F32, name="gate_b", align_bytes=64)
+        gate_a_raw = keep.tile([P, PACK], F32, name="gate_a_raw")
+        gate_b_raw = keep.tile([P, PACK], F32, name="gate_b_raw", tag="wb_scale", align_bytes=64)
+        wb_scale = keep.tile([P, PACK, P], U8, name="wb_scale", tag="wb_scale", align_bytes=64)
+        identity = keep.tile([P, P], F32, name="identity")
         za = [keep.tile([P, S], F32, name=f"za{t}", align_bytes=64) for t in range(PACK)]
-        zb = [keep.tile([P, S], F32, name=f"zb{t}", align_bytes=64) for t in range(PACK)]
+        zb = [keep.tile([P, 2 * S], F32, name=f"zb{t}", align_bytes=64) for t in range(PACK)]
         ya = [keep.tile([P, PACK, w], F32, name=f"ya{c}", align_bytes=64) for c, (a, w) in enumerate(CHUNKS)]
-        yb = [keep.tile([P, PACK, w], F32, name=f"yb{c}", align_bytes=64) for c, (a, w) in enumerate(CHUNKS)]
+        yb = keep.tile([P, PACK, T], F32, name="yb", align_bytes=64)
         y = [keep.tile([P, PACK, w], F32, name=f"y{c}", align_bytes=64) for c, (a, w) in enumerate(CHUNKS)]
         y_bf = [keep.tile([P, w, PACK], BF16, name=f"y_bf{c}", align_bytes=64) for c, (a, w) in enumerate(CHUNKS)]
         y_codes = keep.tile([P, T], I32, name="y_codes", align_bytes=64)
         y_scale = keep.tile([P, T], U8, name="y_scale", align_bytes=64)
         first_half = psum.tile([P, S], F32, name="first_half", tag="bank_a3")
-        whole_b = [psum.tile([P, S], F32, name=f"bank_b{t}") for t in range(PACK)]
+        gate_b_bank = psum.tile([P, PACK, P], F32, name="gate_b_bank", tag="bank_a2")
+        whole_b = [psum.tile([P, S], F32, name=f"bank_b{t}", tag=f"bank_b{t}") for t in range(PACK)]
         bank_b = [[whole_b[t][:, 0:HALF], whole_b[t][:, HALF:S]] for t in range(PACK)]
         bank_b[0] = [first_half[:, 0:HALF], whole_b[0][:, HALF:S]]
+        gate_a_bank = psum.tile([P, PACK, P], F32, name="gate_a_bank", tag="bank_b0")
         bank_a = [psum.tile([P, S], F32, name=f"bank_a{t}", tag=f"bank_a{t}") for t in range(PACK)]
 
-        for plane in (wb_scale_raw, wa_scale_raw, xa_scale):
+        nc.gpsimd.memset(wb_scale_raw[:].bitcast(I32), 0)
+        for plane in (wa_scale_raw, xa_scale):
             nc.vector.memset(plane[:].bitcast(I32), 0)
 
+        make_identity(nc, identity[:])
+        nc.gpsimd.dma_start(out=gate_a_raw[:], in_=ga[0].rearrange("(p c) -> p c", c=PACK))
+
         xb_rows = xb.rearrange("(p j) s -> p j s", j=PACK)
+        nc.sync.dma_start(out=gate_b_raw[:], in_=gb[0].rearrange("(p c) -> p c", c=PACK))
         nc.sync.dma_start(out=xb_raw[0][:], in_=xb_rows[:, :, 0:HALF])
         nc.sync.dma_start(out=wb_raw[:].bitcast(I32), in_=wb_words[0].bitcast(I32))
         load_scale_rows(nc, wb_scale_raw, wb_scales)
@@ -82,11 +97,14 @@ def tile_moe_heads_combine_two_buffers_pl_kernel(
         nc.sync.dma_start(lists_b[:], offs2)
         nc.sync.dma_start(out=wa_raw[:], in_=wa_words.rearrange("z p c r -> p z (c r)").bitcast(I32))
         load_scale_rows(nc, wa_scale_raw, wa_scales)
-        nc.sync.dma_start(out=gate_b[:], in_=gb[0].partition_broadcast(P))
         nc.sync.dma_start(out=xa_codes[:].bitcast(I32), in_=xa_words.rearrange("z p c -> p z c").bitcast(I32))
         load_scale_rows(nc, xa_scale, xa_scales)
         nc.sync.dma_start(lists_a[:], offs)
-        nc.sync.dma_start(out=gate_a[:], in_=ga[0].partition_broadcast(P))
+
+        def spread_gate(gate, raw, bank):
+            for c in range(PACK):
+                nc.tensor.transpose(bank[:, c, :], raw[:, c : c + 1].to_broadcast([P, P]), identity[:])
+            nc.scalar.copy(out=gate[:].rearrange("p (n c) -> p n c", c=PACK), in_=bank[:].rearrange("p c n -> p n c"))
 
         def round_xb(h, lo, hi, copy):
             copy(
@@ -135,7 +153,7 @@ def tile_moe_heads_combine_two_buffers_pl_kernel(
 
         def combine(c):
             a, w = CHUNKS[c]
-            nc.vector.tensor_tensor(y[c][:], ya[c][:], yb[c][:], ADD)
+            nc.vector.tensor_tensor(y[c][:], ya[c][:], yb[:, :, a : a + w], ADD)
             nc.sync.dma_start(out=out_0.rearrange("(p t) c -> p t c", t=PACK)[:, :, a : a + w], in_=y[c][:])
             nc.scalar.copy(
                 out=y_bf[c][:].rearrange("p (c i) t -> p c t i", i=4),
@@ -158,6 +176,7 @@ def tile_moe_heads_combine_two_buffers_pl_kernel(
                 out=out_1[0].rearrange("p c r -> p (c r)").bitcast(I32)[:, a : a + w], in_=y_codes[:, a : a + w]
             )
 
+        spread_gate(gate_b, gate_b_raw, gate_b_bank)
         round_xb(0, 0, HALF, nc.vector.tensor_copy)
         nc.vector.tensor_copy(
             out=wb_codes[:].bitcast(U16).rearrange("p t (c i) -> p c t i", i=8),
@@ -168,17 +187,18 @@ def tile_moe_heads_combine_two_buffers_pl_kernel(
             out=wb_scale[:].rearrange("p t (c i) -> p c t i", i=16),
             in_=wb_scale_raw[:, 0, :].rearrange("p (c i t) -> p c t i", i=16, t=PACK),
         )
-        for t in range(PACK):
-            product_b(t, 0)
+        product_b(0, 0)
         round_xb(1, 0, VECTOR_SHARE, nc.vector.tensor_copy)
         round_xb(1, VECTOR_SHARE, HALF, nc.scalar.copy)
         nc.scalar.copy(out=zb[0][:, 0:HALF], in_=bank_b[0][0])
         quantize_xb(1)
-        for t in range(PACK):
-            product_b(t, 1)
+        product_b(0, 1)
         nc.scalar.copy(out=zb[0][:, HALF:S], in_=bank_b[0][1])
         for t in range(1, PACK):
-            nc.scalar.copy(out=zb[t][:], in_=whole_b[t][:])
+            product_b(t, 0)
+            product_b(t, 1)
+            nc.scalar.copy(out=zb[t][:, 0:S], in_=whole_b[t][:])
+        spread_gate(gate_a, gate_a_raw, gate_a_bank)
         nc.vector.tensor_copy(
             out=wa_codes[:].rearrange("p t z (c i) -> p z c t i", i=4),
             in_=wa_raw[:].rearrange("p z (c i t) -> p z c t i", i=4, t=PACK),
@@ -190,8 +210,7 @@ def tile_moe_heads_combine_two_buffers_pl_kernel(
         for t in range(PACK):
             product_a(t)
         for t in range(PACK):
-            for c in range(len(CHUNKS)):
-                look_up(yb, zb, lists_b, gate_b, c, t)
+            nc.vector.tensor_tensor(yb[:, t, :], zb[t][:].indirect(lists_b[:]), gate_b[:], MULT)
         for c in range(len(CHUNKS)):
             for t in range(PACK):
                 look_up(ya, za, lists_a, gate_a, c, t)

@@ -67,7 +67,10 @@ def tile_moe_heads_combine_two_buffers_pl_kernel(
         identity = keep.tile([P, P], F32, name="identity")
         za = [keep.tile([P, S], F32, name=f"za{t}", align_bytes=64) for t in range(PACK)]
         zb = [keep.tile([P, 2 * S], F32, name=f"zb{t}", align_bytes=64) for t in range(PACK)]
-        ya = [keep.tile([P, PACK, w], F32, name=f"ya{c}", align_bytes=64) for c, (a, w) in enumerate(CHUNKS)]
+        ya_low = keep.tile([P, 2, CHUNKS[0][1]], F32, name="ya_low", tag="ya_low", align_bytes=64)
+        ya_high = keep.tile([P, 2, CHUNKS[0][1]], F32, name="ya_high", align_bytes=64)
+        ya_last = keep.tile([P, PACK, CHUNKS[1][1]], F32, name="ya_last", tag="ya_low", align_bytes=64)
+        ya = [[(0, 2, ya_low), (2, 2, ya_high)], [(0, PACK, ya_last)]]
         yb = keep.tile([P, PACK, T], F32, name="yb", align_bytes=64)
         y = [keep.tile([P, PACK, w], F32, name=f"y{c}", align_bytes=64) for c, (a, w) in enumerate(CHUNKS)]
         y_bf = [keep.tile([P, w, PACK], BF16, name=f"y_bf{c}", align_bytes=64) for c, (a, w) in enumerate(CHUNKS)]
@@ -145,15 +148,15 @@ def tile_moe_heads_combine_two_buffers_pl_kernel(
                 stop=True,
             )
 
-        def look_up(dst, table, lists, gate, c, t):
-            a, w = CHUNKS[c]
-            nc.vector.tensor_tensor(
-                dst[c][:, t, :], table[t][:].indirect(lists[:, a // 16 : (a + w) // 16]), gate[:, a : a + w], MULT
-            )
-
         def combine(c):
             a, w = CHUNKS[c]
-            nc.vector.tensor_tensor(y[c][:], ya[c][:], yb[:, :, a : a + w], ADD)
+            offsets = lists_a[:, a // 16 : (a + w) // 16]
+            for first, count, part in ya[c]:
+                for u in range(count):
+                    nc.vector.tensor_tensor(part[:, u, :], za[first + u][:].indirect(offsets), gate_a[:, a : a + w], MULT)
+            for first, count, part in ya[c]:
+                rows = slice(first, first + count)
+                nc.vector.tensor_tensor(y[c][:, rows, :], part[:], yb[:, rows, a : a + w], ADD)
             nc.sync.dma_start(out=out_0.rearrange("(p t) c -> p t c", t=PACK)[:, :, a : a + w], in_=y[c][:])
             nc.scalar.copy(
                 out=y_bf[c][:].rearrange("p (c i) t -> p c t i", i=4),
@@ -177,7 +180,8 @@ def tile_moe_heads_combine_two_buffers_pl_kernel(
             )
 
         spread_gate(gate_b, gate_b_raw, gate_b_bank)
-        round_xb(0, 0, HALF, nc.vector.tensor_copy)
+        round_xb(0, 0, VECTOR_SHARE, nc.vector.tensor_copy)
+        round_xb(0, VECTOR_SHARE, HALF, nc.scalar.copy)
         nc.vector.tensor_copy(
             out=wb_codes[:].bitcast(U16).rearrange("p t (c i) -> p c t i", i=8),
             in_=wb_raw[:].bitcast(U16).rearrange("p (c i t) -> p c t i", i=8, t=PACK),
@@ -212,8 +216,6 @@ def tile_moe_heads_combine_two_buffers_pl_kernel(
         for t in range(PACK):
             nc.vector.tensor_tensor(yb[:, t, :], zb[t][:].indirect(lists_b[:]), gate_b[:], MULT)
         for c in range(len(CHUNKS)):
-            for t in range(PACK):
-                look_up(ya, za, lists_a, gate_a, c, t)
             combine(c)
         for c in range(len(CHUNKS)):
             quantize_y(c)

from contextlib import ExitStack

import concourse.mybir as mybir
from concourse.masks import make_identity

F32 = mybir.dt.float32
BF16 = mybir.dt.bfloat16
I32 = mybir.dt.int32
U16 = mybir.dt.uint16
U8 = mybir.dt.uint8
FP8X4 = mybir.dt.float8_e4m3fn_x4
FP4X4 = mybir.dt.float4_e2m1fn_x4
MULT = mybir.AluOpType.mult
ADD = mybir.AluOpType.add

P = 128
PACK = 4
K, L, S, T, N = 1024, 512, 512, 512, 512
PASSES_A = K // (P * PACK)
HALF = S // 2
VECTOR_SHARE = 160
CHUNKS = ((0, 384), (384, 128))

FLOPS = 2 * (K + L) * S * N


def load_scale_rows(nc, plane, scales):
    for q in range(4):
        nc.sync.dma_start(
            out=plane[32 * q : 32 * q + 4, :, :].bitcast(I32),
            in_=scales[:, 4 * q : 4 * q + 4, :].rearrange("z r c -> r z c").bitcast(I32),
        )


def tile_moe_heads_combine_two_buffers_pl_kernel(
    tc, xa_words, xa_scales, wa_words, wa_scales, xb, wb_words, wb_scales, ga, gb, offs, offs2, out_0, out_1, out_2
):
    nc = tc.nc
    with ExitStack() as ctx:
        keep = ctx.enter_context(tc.tile_pool(name="keep", bufs=1))
        reuse = ctx.enter_context(tc.tile_pool(name="reuse", bufs=1))
        psum = ctx.enter_context(tc.psum_pool(name="psum", bufs=1))

        lists_a = keep.tile([P, T // 16], U16, name="lists_a")
        lists_b = keep.tile([P, T // 16], U16, name="lists_b")
        wa_raw = keep.tile([P, PASSES_A, N], I32, name="wa_raw", align_bytes=64)
        wa_scale_raw = keep.tile([P, PASSES_A, N], U8, name="wa_scale_raw", align_bytes=64)
        xa_codes = keep.tile([P, PASSES_A, 2 * S], U8, name="xa_codes", align_bytes=64)
        xa_scale = keep.tile([P, PASSES_A, S], U8, name="xa_scale", align_bytes=64)
        wb_raw = keep.tile([P, 2 * N], U8, name="wb_raw", align_bytes=64)
        wb_scale_raw = reuse.tile([P, 1, N], U8, name="wb_scale_raw", align_bytes=64, offset=0)
        wb_codes = keep.tile([P, PACK, 2 * P], U8, name="wb_codes", align_bytes=64)
        xb_raw = [keep.tile([P, PACK, HALF], F32, name=f"xb_raw{h}", align_bytes=64) for h in range(2)]
        xb_bf = [
            keep.tile([P, HALF, PACK], BF16, name="xb_bf0", align_bytes=64),
            reuse.tile([P, HALF, PACK], BF16, name="xb_bf1", align_bytes=64, offset=0),
        ]
        wa_scale = reuse.tile([P, PACK, PASSES_A, P], U8, name="wa_scale", align_bytes=64, offset=0)
        wa_codes = reuse.tile([P, PACK, PASSES_A, P], I32, name="wa_codes", align_bytes=64, offset=1024)
        xb_codes = keep.tile([P, S], I32, name="xb_codes", align_bytes=64)
        xb_scale = keep.tile([P, S], U8, name="xb_scale", align_bytes=64)
        gate_a = keep.tile([P, T], F32, name="gate_a", align_bytes=64)
        gate_b = keep.tile([P, T], F32, name="gate_b", align_bytes=64)
        gate_a_raw = keep.tile([P, PACK], F32, name="gate_a_raw")
        gate_b_raw = keep.tile([P, PACK], F32, name="gate_b_raw", tag="wb_scale", align_bytes=64)
        wb_scale = keep.tile([P, PACK, P], U8, name="wb_scale", tag="wb_scale", align_bytes=64)
        identity = keep.tile([P, P], F32, name="identity")
        za = [keep.tile([P, S], F32, name=f"za{t}", align_bytes=64) for t in range(PACK)]
        zb = [keep.tile([P, 2 * S], F32, name=f"zb{t}", align_bytes=64) for t in range(PACK)]
        ya_low = keep.tile([P, 2, CHUNKS[0][1]], F32, name="ya_low", tag="ya_low", align_bytes=64)
        ya_high = keep.tile([P, 2, CHUNKS[0][1]], F32, name="ya_high", align_bytes=64)
        ya_last = keep.tile([P, PACK, CHUNKS[1][1]], F32, name="ya_last", tag="ya_low", align_bytes=64)
        ya = [[(0, 2, ya_low), (2, 2, ya_high)], [(0, PACK, ya_last)]]
        yb = keep.tile([P, PACK, T], F32, name="yb", align_bytes=64)
        y = [keep.tile([P, PACK, w], F32, name=f"y{c}", align_bytes=64) for c, (a, w) in enumerate(CHUNKS)]
        y_bf = [keep.tile([P, w, PACK], BF16, name=f"y_bf{c}", align_bytes=64) for c, (a, w) in enumerate(CHUNKS)]
        y_codes = keep.tile([P, T], I32, name="y_codes", align_bytes=64)
        y_scale = keep.tile([P, T], U8, name="y_scale", align_bytes=64)
        first_half = psum.tile([P, S], F32, name="first_half", tag="bank_a3")
        gate_b_bank = psum.tile([P, PACK, P], F32, name="gate_b_bank", tag="bank_a2")
        whole_b = [psum.tile([P, S], F32, name=f"bank_b{t}", tag=f"bank_b{t}") for t in range(PACK)]
        bank_b = [[whole_b[t][:, 0:HALF], whole_b[t][:, HALF:S]] for t in range(PACK)]
        bank_b[0] = [first_half[:, 0:HALF], whole_b[0][:, HALF:S]]
        gate_a_bank = psum.tile([P, PACK, P], F32, name="gate_a_bank", tag="bank_b0")
        bank_a = [psum.tile([P, S], F32, name=f"bank_a{t}", tag=f"bank_a{t}") for t in range(PACK)]

        nc.gpsimd.memset(wb_scale_raw[:].bitcast(I32), 0)
        for plane in (wa_scale_raw, xa_scale):
            nc.vector.memset(plane[:].bitcast(I32), 0)

        make_identity(nc, identity[:])
        nc.gpsimd.dma_start(out=gate_a_raw[:], in_=ga[0].rearrange("(p c) -> p c", c=PACK))

        xb_rows = xb.rearrange("(p j) s -> p j s", j=PACK)
        nc.sync.dma_start(out=gate_b_raw[:], in_=gb[0].rearrange("(p c) -> p c", c=PACK))
        nc.sync.dma_start(out=xb_raw[0][:], in_=xb_rows[:, :, 0:HALF])
        nc.sync.dma_start(out=wb_raw[:].bitcast(I32), in_=wb_words[0].bitcast(I32))
        load_scale_rows(nc, wb_scale_raw, wb_scales)
        nc.sync.dma_start(out=xb_raw[1][:], in_=xb_rows[:, :, HALF:S])
        nc.sync.dma_start(lists_b[:], offs2)
        nc.sync.dma_start(out=wa_raw[:], in_=wa_words.rearrange("z p c r -> p z (c r)").bitcast(I32))
        load_scale_rows(nc, wa_scale_raw, wa_scales)
        nc.sync.dma_start(out=xa_codes[:].bitcast(I32), in_=xa_words.rearrange("z p c -> p z c").bitcast(I32))
        load_scale_rows(nc, xa_scale, xa_scales)
        nc.sync.dma_start(lists_a[:], offs)

        def spread_gate(gate, raw, bank):
            for c in range(PACK):
                nc.tensor.transpose(bank[:, c, :], raw[:, c : c + 1].to_broadcast([P, P]), identity[:])
            nc.scalar.copy(out=gate[:].rearrange("p (n c) -> p n c", c=PACK), in_=bank[:].rearrange("p c n -> p n c"))

        def round_xb(h, lo, hi, copy):
            copy(
                out=xb_bf[h][:, lo:hi, :].rearrange("p (c i) j -> p c j i", i=4),
                in_=xb_raw[h][:, :, lo:hi].rearrange("p j (c i) -> p c j i", i=4),
            )

        def quantize_xb(h):
            cols = slice(h * HALF, (h + 1) * HALF)
            nc.vector.quantize_mx(
                out=xb_codes[:, cols].bitcast(FP8X4),
                scales=xb_scale[:, cols],
                in_=xb_bf[h][:].rearrange("p s j -> p (s j)"),
            )

        def product_a(t):
            for z in range(PASSES_A):
                nc.tensor.matmul_mx(
                    out=bank_a[t][:],
                    lhsT=wa_codes[:, t, z, :].bitcast(FP8X4),
                    lhsT_scale=wa_scale[:, t, z, :],
                    rhs=xa_codes[:, z, :].bitcast(FP4X4),
                    rhs_scale=xa_scale[:, z, :],
                    start=(z == 0),
                    stop=(z == PASSES_A - 1),
                )
            nc.scalar.copy(out=za[t][:], in_=bank_a[t][:])

        def product_b(t, h):
            cols = slice(h * HALF, (h + 1) * HALF)
            nc.tensor.matmul_mx(
                out=bank_b[t][h],
                lhsT=wb_codes[:, t, :].bitcast(FP4X4),
                lhsT_scale=wb_scale[:, t, :],
                rhs=xb_codes[:, cols].bitcast(FP8X4),
                rhs_scale=xb_scale[:, cols],
                start=True,
                stop=True,
            )

        def combine(c):
            a, w = CHUNKS[c]
            offsets = lists_a[:, a // 16 : (a + w) // 16]
            for first, count, part in ya[c]:
                for u in range(count):
                    nc.vector.tensor_tensor(part[:, u, :], za[first + u][:].indirect(offsets), gate_a[:, a : a + w], MULT)
            for first, count, part in ya[c]:
                rows = slice(first, first + count)
                nc.vector.tensor_tensor(y[c][:, rows, :], part[:], yb[:, rows, a : a + w], ADD)
            nc.sync.dma_start(out=out_0.rearrange("(p t) c -> p t c", t=PACK)[:, :, a : a + w], in_=y[c][:])
            nc.scalar.copy(
                out=y_bf[c][:].rearrange("p (c i) t -> p c t i", i=4),
                in_=y[c][:].rearrange("p t (c i) -> p c t i", i=4),
            )

        def quantize_y(c):
            a, w = CHUNKS[c]
            flat = y_bf[c][:].rearrange("p c t -> p (c t)")
            lo = 0
            while lo < w:
                n = 256 if w - lo >= 256 else 128
                nc.vector.quantize_mx(
                    out=y_codes[:, a + lo : a + lo + n].bitcast(FP8X4),
                    scales=y_scale[:, a + lo : a + lo + n],
                    in_=flat[:, PACK * lo : PACK * (lo + n)],
                )
                lo = lo + n
            nc.sync.dma_start(
                out=out_1[0].rearrange("p c r -> p (c r)").bitcast(I32)[:, a : a + w], in_=y_codes[:, a : a + w]
            )

        spread_gate(gate_b, gate_b_raw, gate_b_bank)
        round_xb(0, 0, VECTOR_SHARE, nc.vector.tensor_copy)
        round_xb(0, VECTOR_SHARE, HALF, nc.scalar.copy)
        nc.vector.tensor_copy(
            out=wb_codes[:].bitcast(U16).rearrange("p t (c i) -> p c t i", i=8),
            in_=wb_raw[:].bitcast(U16).rearrange("p (c i t) -> p c t i", i=8, t=PACK),
        )
        quantize_xb(0)
        nc.vector.tensor_copy(
            out=wb_scale[:].rearrange("p t (c i) -> p c t i", i=16),
            in_=wb_scale_raw[:, 0, :].rearrange("p (c i t) -> p c t i", i=16, t=PACK),
        )
        product_b(0, 0)
        round_xb(1, 0, VECTOR_SHARE, nc.vector.tensor_copy)
        round_xb(1, VECTOR_SHARE, HALF, nc.scalar.copy)
        nc.scalar.copy(out=zb[0][:, 0:HALF], in_=bank_b[0][0])
        quantize_xb(1)
        product_b(0, 1)
        nc.scalar.copy(out=zb[0][:, HALF:S], in_=bank_b[0][1])
        for t in range(1, PACK):
            product_b(t, 0)
            product_b(t, 1)
            nc.scalar.copy(out=zb[t][:, 0:S], in_=whole_b[t][:])
        spread_gate(gate_a, gate_a_raw, gate_a_bank)
        nc.vector.tensor_copy(
            out=wa_codes[:].rearrange("p t z (c i) -> p z c t i", i=4),
            in_=wa_raw[:].rearrange("p z (c i t) -> p z c t i", i=4, t=PACK),
        )
        nc.vector.tensor_copy(
            out=wa_scale[:].rearrange("p t z (c i) -> p z c t i", i=16),
            in_=wa_scale_raw[:].rearrange("p z (c i t) -> p z c t i", i=16, t=PACK),
        )
        for t in range(PACK):
            product_a(t)
        for t in range(PACK):
            nc.vector.tensor_tensor(yb[:, t, :], zb[t][:].indirect(lists_b[:]), gate_b[:], MULT)
        for c in range(len(CHUNKS)):
            combine(c)
        for c in range(len(CHUNKS)):
            quantize_y(c)
        for q in range(4):
            queue = nc.scalar if q % 2 else nc.sync
            queue.dma_start(
                out=out_2[0, 4 * q : 4 * q + 4, :].bitcast(I32), in_=y_scale[32 * q : 32 * q + 4, :].bitcast(I32)
            )
